import numpy as np
import ml_dtypes


def mxq(x, axis, fmt="e4m3"):
    dtype, down = {"e4m3": (ml_dtypes.float8_e4m3fn, 7), "e5m2": (ml_dtypes.float8_e5m2, 14)}[fmt]
    v = np.moveaxis(np.asarray(x, np.float32).astype(ml_dtypes.bfloat16).astype(np.float64), axis, -1)
    blocks = v.reshape(v.shape[:-1] + (-1, 32))
    amax = np.abs(blocks).max(-1, keepdims=True)
    byte = np.maximum(np.where(amax > 0, np.frexp(amax)[1] - 1 + 127, 0) - down, 1)
    scale = np.exp2(byte - 127.0)
    codes = (blocks / scale).astype(np.float32).astype(dtype).astype(np.float64)
    return np.moveaxis((codes * scale).reshape(v.shape), -1, axis)


WIDE = False


def mx_kscale(k):
    if not WIDE:
        return np.ones(k)
    levels = np.array([30, -30])
    if k % 512:
        return np.exp2(np.random.permutation(np.resize(levels, k // 32))).repeat(32)
    a = np.empty((k // 512, 16))
    for p in range(k // 512):
        a[p, :8] = np.random.permutation(np.resize(levels, 8))
        for g in range(8):
            far = levels[np.abs(levels - a[p, g]) >= 10]
            a[p, g + 8] = far[np.random.randint(len(far))]
    return np.exp2(a.ravel()).repeat(32)


def f64(x):
    return np.asarray(x).astype(np.float64)


def striped(idx):
    return np.tile(np.asarray(idx).reshape(-1, 16).T, (8, 1)).astype(np.uint16)


def unstriped(offs):
    return offs[:16].T.reshape(-1).astype(np.int64)


E2M1 = np.array([0.0, 0.5, 1.0, 1.5, 2.0, 3.0, 4.0, 6.0, -0.0, -0.5, -1.0, -1.5, -2.0, -3.0, -4.0, -6.0])


def pack_weight(w, fmt):
    k, n = w.shape
    w = f64(np.asarray(w, np.float32).astype(ml_dtypes.bfloat16)).reshape(k // 32, 32, n)
    amax = np.abs(w).max(1)
    if fmt == "e4m3":
        byte = np.frexp(amax)[1] - 1 + 127 - 7
    else:
        mant, ex = np.frexp(amax / 6.0)
        byte = np.where(mant > 0.5, ex, ex - 1) + 127
    byte = np.clip(np.where(amax > 0, byte, 1), 1, 254)
    scaled = (w * np.exp2(127.0 - byte)[:, None, :]).reshape(k, n).astype(np.float32)
    by_word = np.ascontiguousarray(scaled.reshape(k // 512, 128, 4, n).transpose(0, 1, 3, 2))
    if fmt == "e4m3":
        words = by_word.astype(ml_dtypes.float8_e4m3fn).view(np.uint8)
    else:
        c = by_word.astype(ml_dtypes.float4_e2m1fn).view(np.uint8) & 0xF
        words = (c[..., 0::2] | (c[..., 1::2] << 4)).reshape(k // 512, 128, 2 * n)
    return np.ascontiguousarray(words), np.ascontiguousarray(byte.astype(np.uint8).reshape(k // 512, 16, n))


def unpack_weight(words, scales, fmt):
    g, _, n = scales.shape
    words = np.ascontiguousarray(words).reshape(g, 128, n, -1)
    if fmt == "e4m3":
        vals = words.view(ml_dtypes.float8_e4m3fn).astype(np.float64)
    else:
        nib = np.empty((g, 128, n, 4), np.uint8)
        nib[..., 0::2] = words & 0xF
        nib[..., 1::2] = words >> 4
        vals = E2M1[nib]
    vals = vals * np.repeat(np.exp2(scales.astype(np.float64) - 127.0), 8, axis=1)[..., None]
    return vals.transpose(0, 1, 3, 2).reshape(g * 512, n)


def bf(x):
    return np.asarray(x, np.float32).astype(ml_dtypes.bfloat16)


def planes(Y):
    r, m = Y.shape
    b = f64(bf(Y)).reshape(r // 32, 32, m)
    amax = np.abs(b).max(1)
    byte = np.clip(np.where(amax > 0, np.frexp(amax)[1] - 1 + 127 - 7, 1), 1, 254)
    codes = (b * np.exp2(127.0 - byte)[:, None, :]).reshape(r, m).astype(np.float32).astype(ml_dtypes.float8_e4m3fn).view(np.uint8)
    words = codes.reshape(r // 512, 128, 4, m).transpose(0, 1, 3, 2)
    return np.ascontiguousarray(words), np.ascontiguousarray(byte.astype(np.uint8).reshape(r // 512, 16, m))


K, N, M, T, J = 512, 512, 512, 512, 512


def setup_inputs():
    n = np.random.standard_normal
    idx = np.random.randint(0, T, J)
    fk = mx_kscale(K)
    fn = mx_kscale(N)
    xtp = pack_weight(n((K, T)) / fk[:, None], "e2m1")
    wp = pack_weight(n((K, N)) * 1 / np.sqrt(K) * fk[:, None] * fn, "e4m3")
    wbp = pack_weight(n((N, M)) * 1 / np.sqrt(N) / fn[:, None], "e2m1")
    return {
        "xt_words": xtp[0],
        "xt_scales": xtp[1],
        "w_words": wp[0],
        "w_scales": wp[1],
        "g": (1.0 * n((N, J))).astype(np.float32),
        "wb_words": wbp[0],
        "wb_scales": wbp[1],
        "offs": striped(idx),
    }


def reference(xt_words, xt_scales, w_words, w_scales, g, wb_words, wb_scales, offs):
    idx = unstriped(offs)
    xtu = unpack_weight(xt_words, xt_scales, "e2m1")
    wu = unpack_weight(w_words, w_scales, "e4m3")
    wbu = unpack_weight(wb_words, wb_scales, "e2m1")
    z = wu.T @ xtu
    d = f64(g) * z[:, idx]
    dq = mxq(d, 0, "e5m2")
    y = wbu.T @ dq
    words, scales = planes(y)
    return y, words, scales

@@ -1,0 +1,182 @@
+from contextlib import ExitStack
+
+import concourse.mybir as mybir
+
+K, N, M, T, J = 512, 512, 512, 512, 512
+FLOPS = 2 * K * N * T + 2 * N * M * J
+
+F32 = mybir.dt.float32
+BF16 = mybir.dt.bfloat16
+I32 = mybir.dt.int32
+U32 = mybir.dt.uint32
+U16 = mybir.dt.uint16
+U8 = mybir.dt.uint8
+E4M3X4 = mybir.dt.float8_e4m3fn_x4
+E5M2X4 = mybir.dt.float8_e5m2_x4
+E2M1X4 = mybir.dt.float4_e2m1fn_x4
+MULT = mybir.AluOpType.mult
+
+P = 128
+PACK = 4
+QUADS = 4
+LIST_ROWS = 16
+PIECES = ((0, 256), (256, 384), (384, 512))
+G_LOADS = ((0, 2, 0, 256), (2, 4, 0, 256), (0, 4, 256, 512))
+Y_HALF = 256
+Y_SPLIT = 352
+
+
+def scale_rows(tile, quad):
+    return tile[32 * quad : 32 * quad + 4, :].bitcast(I32)
+
+
+def interleave(copy, dst, src):
+    copy(
+        out=dst.rearrange("p (c i) t -> p c t i", i=4),
+        in_=src.rearrange("p t (c i) -> p c t i", i=4),
+    )
+
+
+def tile_list_pair_product_back_pl_kernel(
+    tc, xt_words, xt_scales, w_words, w_scales, g, wb_words, wb_scales, offs, out_0, out_1, out_2
+):
+    nc = tc.nc
+    with ExitStack() as ctx:
+        keep = ctx.enter_context(tc.tile_pool(name="keep", bufs=1))
+        psum = ctx.enter_context(tc.psum_pool(name="psum", bufs=1))
+
+        def sb(name, shape, dtype):
+            return keep.tile(shape, dtype, name=name, align_bytes=64)
+
+        offsets = keep.tile([P, J // LIST_ROWS], U16, name="offsets")
+        w_raw = sb("w_raw", [P, N], I32)
+        xt_codes = sb("xt_codes", [P, 2 * T], U8)
+        wb_raw = sb("wb_raw", [P, 2 * M], U8)
+        w_sc_raw = sb("w_sc_raw", [P, N], U8)
+        xt_sc = sb("xt_sc", [P, T], U8)
+        wb_sc_raw = sb("wb_sc_raw", [P, M], U8)
+        for plane in (w_sc_raw, xt_sc, wb_sc_raw):
+            nc.vector.memset(plane[:].bitcast(I32), 0)
+
+        def load_scales(queue, plane, src, quad):
+            queue.dma_start(out=scale_rows(plane, quad), in_=src[0].bitcast(I32)[4 * quad : 4 * quad + 4, :])
+
+        nc.sync.dma_start(out=w_raw[:], in_=w_words[0].rearrange("p n t -> p (n t)").bitcast(I32))
+        nc.scalar.dma_start(out=xt_codes[:].bitcast(I32), in_=xt_words[0].bitcast(I32))
+        for quad in range(QUADS):
+            load_scales(nc.sync if quad % 2 == 0 else nc.scalar, w_sc_raw, w_scales, quad)
+        for quad in range(QUADS):
+            load_scales(nc.scalar if quad == 1 else nc.sync, xt_sc, xt_scales, quad)
+        nc.sync.dma_start(out=wb_raw[:].bitcast(I32), in_=wb_words[0].bitcast(I32))
+        g_rows = g.rearrange("(p r) j -> p r j", r=PACK)
+        g_tiles = []
+        for r0, r1, j0, j1 in G_LOADS:
+            g_part = sb("g_%d_%d" % (r0, j0), [P, r1 - r0, j1 - j0], F32)
+            nc.sync.dma_start(out=g_part[:], in_=g_rows[:, r0:r1, j0:j1])
+            g_tiles.append(g_part)
+            if len(g_tiles) == 1:
+                nc.sync.dma_start(offsets[:], offs)
+        for quad in range(QUADS):
+            load_scales(nc.sync, wb_sc_raw, wb_scales, quad)
+
+        def g_slice(r, a, b):
+            for (r0, r1, j0, j1), g_part in zip(G_LOADS, g_tiles):
+                if r0 <= r < r1 and j0 <= a and b <= j1:
+                    return g_part[:, r - r0, a - j0 : b - j0]
+            raise ValueError("no load holds this part of g")
+
+        w_codes = sb("w_codes", [P, PACK, P], I32)
+        w_sc = sb("w_sc", [P, PACK, P], U8)
+        nc.vector.tensor_copy(
+            out=w_sc[:].rearrange("p r q -> p q r"), in_=w_sc_raw[:].rearrange("p (q r) -> p q r", r=PACK)
+        )
+        nc.vector.tensor_copy(
+            out=w_codes[:].rearrange("p r q -> p q r"), in_=w_raw[:].rearrange("p (q r) -> p q r", r=PACK)
+        )
+
+        z_tiles = []
+        for r in range(PACK):
+            z_bank = psum.tile([P, T], F32, name="z_bank%d" % r)
+            nc.tensor.matmul_mx(
+                out=z_bank[:],
+                lhsT=w_codes[:, r, :].bitcast(E4M3X4),
+                lhsT_scale=w_sc[:, r, :],
+                rhs=xt_codes[:].bitcast(E2M1X4),
+                rhs_scale=xt_sc[:],
+                start=True,
+                stop=True,
+            )
+            z = sb("z%d" % r, [P, T], F32)
+            nc.scalar.copy(out=z[:], in_=z_bank[:])
+            z_tiles.append(z)
+
+        wb_codes = sb("wb_codes", [P, PACK, 2 * P], U8)
+        wb_sc = sb("wb_sc", [P, PACK, P], U8)
+        nc.vector.tensor_copy(
+            out=wb_codes[:].rearrange("p r (q b) -> p q r b", b=2),
+            in_=wb_raw[:].rearrange("p (q r b) -> p q r b", r=PACK, b=2),
+        )
+
+        d_codes = sb("d_codes", [P, J], U32)
+        d_sc = sb("d_sc", [P, J], U8)
+        rounded = []
+        for a, b in PIECES:
+            d = sb("d%d" % a, [P, PACK, b - a], F32)
+            for r in range(PACK):
+                nc.vector.tensor_tensor(
+                    d[:, r, :],
+                    z_tiles[r][:].indirect(offsets[:, a // LIST_ROWS : b // LIST_ROWS]),
+                    g_slice(r, a, b),
+                    MULT,
+                )
+            d_bf = sb("d_bf%d" % a, [P, b - a, PACK], BF16)
+            interleave(nc.scalar.copy, d_bf[:], d[:])
+            rounded.append(d_bf)
+        nc.vector.tensor_copy(
+            out=wb_sc[:].rearrange("p r q -> p q r"), in_=wb_sc_raw[:].rearrange("p (q r) -> p q r", r=PACK)
+        )
+        for (a, b), d_bf in zip(PIECES, rounded):
+            nc.vector.quantize_mx(
+                out=d_codes[:, a:b].bitcast(E5M2X4),
+                scales=d_sc[:, a:b],
+                in_=d_bf[:].rearrange("p j t -> p (j t)"),
+            )
+
+        y = sb("y", [P, PACK, J], F32)
+        out_rows = out_0.rearrange("(p r) j -> p r j", r=PACK)
+        for r in range(PACK):
+            y_bank = psum.tile([P, J], F32, name="y_bank%d" % r)
+            nc.tensor.matmul_mx(
+                out=y_bank[:],
+                lhsT=wb_codes[:, r, :].bitcast(E2M1X4),
+                lhsT_scale=wb_sc[:, r, :],
+                rhs=d_codes[:].bitcast(E5M2X4),
+                rhs_scale=d_sc[:],
+                start=True,
+                stop=True,
+            )
+            if r % 2 == 0:
+                nc.vector.tensor_copy(out=y[:, r, :], in_=y_bank[:])
+            else:
+                nc.scalar.copy(out=y[:, r, :], in_=y_bank[:])
+            nc.sync.dma_start(out=out_rows[:, r, :], in_=y[:, r, :])
+
+        y_bf = [sb("y_bf%d" % h, [P, Y_HALF, PACK], BF16) for h in range(2)]
+        interleave(nc.vector.tensor_copy, y_bf[0][:], y[:, :, 0:Y_HALF])
+        interleave(nc.scalar.copy, y_bf[1][:, Y_SPLIT - Y_HALF :, :], y[:, :, Y_SPLIT:J])
+        interleave(nc.vector.tensor_copy, y_bf[1][:, : Y_SPLIT - Y_HALF, :], y[:, :, Y_HALF:Y_SPLIT])
+
+        y_codes = sb("y_codes", [P, J], U32)
+        y_sc = sb("y_sc", [P, J], U8)
+        words_out = out_1[0].rearrange("p c t -> p (c t)").bitcast(I32)
+        for h in range(2):
+            cols = slice(h * Y_HALF, (h + 1) * Y_HALF)
+            nc.vector.quantize_mx(
+                out=y_codes[:, cols].bitcast(E4M3X4),
+                scales=y_sc[:, cols],
+                in_=y_bf[h][:].rearrange("p j t -> p (j t)"),
+            )
+            nc.sync.dma_start(out=words_out[:, cols], in_=y_codes[:, cols].bitcast(I32))
+        for quad in range(QUADS):
+            queue = nc.scalar if quad < 3 else nc.sync
+            queue.dma_start(out=out_2[0].bitcast(I32)[4 * quad : 4 * quad + 4, :], in_=scale_rows(y_sc, quad))

@@ -20,10 +20,10 @@ P = 128
 PACK = 4
 QUADS = 4
 LIST_ROWS = 16
-PIECES = ((0, 256), (256, 384), (384, 512))
+PIECES = ((0, 256), (256, 384), (384, 448), (448, 512))
 G_LOADS = ((0, 2, 0, 256), (2, 4, 0, 256), (0, 4, 256, 512))
 Y_HALF = 256
-Y_SPLIT = 352
+Y_SPLIT = 96
 
 
 def scale_rows(tile, quad):
@@ -45,8 +45,8 @@ def tile_list_pair_product_back_pl_kernel(
         keep = ctx.enter_context(tc.tile_pool(name="keep", bufs=1))
         psum = ctx.enter_context(tc.psum_pool(name="psum", bufs=1))
 
-        def sb(name, shape, dtype):
-            return keep.tile(shape, dtype, name=name, align_bytes=64)
+        def sb(name, shape, dtype, tag=None):
+            return keep.tile(shape, dtype, name=name, tag=tag or name, align_bytes=64)
 
         offsets = keep.tile([P, J // LIST_ROWS], U16, name="offsets")
         w_raw = sb("w_raw", [P, N], I32)
@@ -66,24 +66,11 @@ def tile_list_pair_product_back_pl_kernel(
         for quad in range(QUADS):
             load_scales(nc.sync if quad % 2 == 0 else nc.scalar, w_sc_raw, w_scales, quad)
         for quad in range(QUADS):
-            load_scales(nc.scalar if quad == 1 else nc.sync, xt_sc, xt_scales, quad)
-        nc.sync.dma_start(out=wb_raw[:].bitcast(I32), in_=wb_words[0].bitcast(I32))
-        g_rows = g.rearrange("(p r) j -> p r j", r=PACK)
-        g_tiles = []
-        for r0, r1, j0, j1 in G_LOADS:
-            g_part = sb("g_%d_%d" % (r0, j0), [P, r1 - r0, j1 - j0], F32)
-            nc.sync.dma_start(out=g_part[:], in_=g_rows[:, r0:r1, j0:j1])
-            g_tiles.append(g_part)
-            if len(g_tiles) == 1:
-                nc.sync.dma_start(offsets[:], offs)
+            load_scales(nc.scalar if quad == 0 else nc.sync, xt_sc, xt_scales, quad)
+        nc.sync.dma_start(offsets[:], offs)
+        nc.gpsimd.dma_start(out=wb_raw[:].bitcast(I32), in_=wb_words[0].bitcast(I32))
         for quad in range(QUADS):
             load_scales(nc.sync, wb_sc_raw, wb_scales, quad)
-
-        def g_slice(r, a, b):
-            for (r0, r1, j0, j1), g_part in zip(G_LOADS, g_tiles):
-                if r0 <= r < r1 and j0 <= a and b <= j1:
-                    return g_part[:, r - r0, a - j0 : b - j0]
-            raise ValueError("no load holds this part of g")
 
         w_codes = sb("w_codes", [P, PACK, P], I32)
         w_sc = sb("w_sc", [P, PACK, P], U8)
@@ -94,23 +81,43 @@ def tile_list_pair_product_back_pl_kernel(
             out=w_codes[:].rearrange("p r q -> p q r"), in_=w_raw[:].rearrange("p (q r) -> p q r", r=PACK)
         )
 
+        g_rows = g.rearrange("(p r) j -> p r j", r=PACK)
+        g_all = sb("g_all", [P, PACK * J], F32, tag="w_raw")
+        g_parts = []
+        start = 0
+        for r0, r1, j0, j1 in G_LOADS:
+            size = (r1 - r0) * (j1 - j0)
+            g_part = g_all[:, start : start + size].rearrange("p (r j) -> p r j", r=r1 - r0)
+            nc.sync.dma_start(out=g_part, in_=g_rows[:, r0:r1, j0:j1])
+            g_parts.append(start)
+            start = start + size
+
+        def g_slice(r, a, b):
+            for (r0, r1, j0, j1), first in zip(G_LOADS, g_parts):
+                if r0 <= r < r1 and j0 <= a and b <= j1:
+                    col = first + (r - r0) * (j1 - j0) + a - j0
+                    return g_all[:, col : col + b - a]
+            raise ValueError("no load holds this part of g")
+
         z_tiles = []
         for r in range(PACK):
-            z_bank = psum.tile([P, T], F32, name="z_bank%d" % r)
-            nc.tensor.matmul_mx(
-                out=z_bank[:],
-                lhsT=w_codes[:, r, :].bitcast(E4M3X4),
-                lhsT_scale=w_sc[:, r, :],
-                rhs=xt_codes[:].bitcast(E2M1X4),
-                rhs_scale=xt_sc[:],
-                start=True,
-                stop=True,
-            )
             z = sb("z%d" % r, [P, T], F32)
-            nc.scalar.copy(out=z[:], in_=z_bank[:])
+            width = T // 2 if r == 0 else T
+            for t0 in range(0, T, width):
+                z_bank = psum.tile([P, width], F32, name="z_bank%d_%d" % (r, t0))
+                nc.tensor.matmul_mx(
+                    out=z_bank[:],
+                    lhsT=w_codes[:, r, :].bitcast(E4M3X4),
+                    lhsT_scale=w_sc[:, r, :],
+                    rhs=xt_codes[:, 2 * t0 : 2 * (t0 + width)].bitcast(E2M1X4),
+                    rhs_scale=xt_sc[:, t0 : t0 + width],
+                    start=True,
+                    stop=True,
+                )
+                nc.scalar.copy(out=z[:, t0 : t0 + width], in_=z_bank[:])
             z_tiles.append(z)
 
-        wb_codes = sb("wb_codes", [P, PACK, 2 * P], U8)
+        wb_codes = sb("wb_codes", [P, PACK, 2 * P], U8, tag="w_sc_raw")
         wb_sc = sb("wb_sc", [P, PACK, P], U8)
         nc.vector.tensor_copy(
             out=wb_codes[:].rearrange("p r (q b) -> p q r b", b=2),
@@ -142,10 +149,13 @@ def tile_list_pair_product_back_pl_kernel(
                 in_=d_bf[:].rearrange("p j t -> p (j t)"),
             )
 
-        y = sb("y", [P, PACK, J], F32)
         out_rows = out_0.rearrange("(p r) j -> p r j", r=PACK)
+        halves = [slice(h * Y_HALF, (h + 1) * Y_HALF) for h in range(2)]
+        y_low = sb("y_low", [P, 2, J], F32)
+        y_high = [sb("y_high%d" % h, [P, 2, Y_HALF], F32) for h in range(2)]
+        y_bf = [sb("y_bf%d" % h, [P, Y_HALF, PACK], BF16) for h in range(2)]
         for r in range(PACK):
-            y_bank = psum.tile([P, J], F32, name="y_bank%d" % r)
+            y_bank = psum.tile([P, J], F32, name="y_bank%d" % r, tag="z_bank0_0" if r == PACK - 1 else "y_bank%d" % r)
             nc.tensor.matmul_mx(
                 out=y_bank[:],
                 lhsT=wb_codes[:, r, :].bitcast(E2M1X4),
@@ -155,16 +165,21 @@ def tile_list_pair_product_back_pl_kernel(
                 start=True,
                 stop=True,
             )
-            if r % 2 == 0:
-                nc.vector.tensor_copy(out=y[:, r, :], in_=y_bank[:])
+            if r < 2:
+                copy = nc.vector.tensor_copy if r == 0 else nc.scalar.copy
+                copy(out=y_low[:, r, :], in_=y_bank[:])
+                nc.sync.dma_start(out=out_rows[:, r, :], in_=y_low[:, r, :])
             else:
-                nc.scalar.copy(out=y[:, r, :], in_=y_bank[:])
-            nc.sync.dma_start(out=out_rows[:, r, :], in_=y[:, r, :])
-
-        y_bf = [sb("y_bf%d" % h, [P, Y_HALF, PACK], BF16) for h in range(2)]
-        interleave(nc.vector.tensor_copy, y_bf[0][:], y[:, :, 0:Y_HALF])
-        interleave(nc.scalar.copy, y_bf[1][:, Y_SPLIT - Y_HALF :, :], y[:, :, Y_SPLIT:J])
-        interleave(nc.vector.tensor_copy, y_bf[1][:, : Y_SPLIT - Y_HALF, :], y[:, :, Y_HALF:Y_SPLIT])
+                for h in range(2):
+                    nc.scalar.copy(out=y_high[h][:, r - 2, :], in_=y_bank[:, halves[h]])
+            if r == 1:
+                for h in range(2):
+                    nc.vector.tensor_copy(out=y_bf[h][:, :, 0:2], in_=y_low[:, :, halves[h]].rearrange("p t j -> p j t"))
+        for h in range(2):
+            nc.sync.dma_start(out=out_rows[:, 2:PACK, halves[h]], in_=y_high[h][:])
+        nc.vector.tensor_copy(out=y_bf[0][:, :, 2:PACK], in_=y_high[0][:].rearrange("p t j -> p j t"))
+        nc.scalar.copy(out=y_bf[1][:, Y_SPLIT:, 2:PACK], in_=y_high[1][:, :, Y_SPLIT:].rearrange("p t j -> p j t"))
+        nc.vector.tensor_copy(out=y_bf[1][:, :Y_SPLIT, 2:PACK], in_=y_high[1][:, :, :Y_SPLIT].rearrange("p t j -> p j t"))
 
         y_codes = sb("y_codes", [P, J], U32)
         y_sc = sb("y_sc", [P, J], U8)

@@ -20,7 +20,7 @@ P = 128
 PACK = 4
 QUADS = 4
 LIST_ROWS = 16
-PIECES = ((0, 256), (256, 384), (384, 448), (448, 512))
+PIECES = ((0, 256), (256, 384), (384, 512))
 G_LOADS = ((0, 2, 0, 256), (2, 4, 0, 256), (0, 4, 256, 512))
 Y_HALF = 256
 Y_SPLIT = 96
@@ -61,16 +61,32 @@ def tile_list_pair_product_back_pl_kernel(
         def load_scales(queue, plane, src, quad):
             queue.dma_start(out=scale_rows(plane, quad), in_=src[0].bitcast(I32)[4 * quad : 4 * quad + 4, :])
 
+        nc.sync.dma_start(out=xt_codes[:].bitcast(I32), in_=xt_words[0].bitcast(I32))
         nc.sync.dma_start(out=w_raw[:], in_=w_words[0].rearrange("p n t -> p (n t)").bitcast(I32))
-        nc.scalar.dma_start(out=xt_codes[:].bitcast(I32), in_=xt_words[0].bitcast(I32))
         for quad in range(QUADS):
-            load_scales(nc.sync if quad % 2 == 0 else nc.scalar, w_sc_raw, w_scales, quad)
+            load_scales(nc.scalar if quad < 3 else nc.sync, w_sc_raw, w_scales, quad)
         for quad in range(QUADS):
             load_scales(nc.scalar if quad == 0 else nc.sync, xt_sc, xt_scales, quad)
+        nc.sync.dma_start(out=wb_raw[:].bitcast(I32), in_=wb_words[0].bitcast(I32))
+        g_rows = g.rearrange("(p r) j -> p r j", r=PACK)
+        g_tiles = [sb("g_%d_%d" % (r0, j0), [P, r1 - r0, j1 - j0], F32) for r0, r1, j0, j1 in G_LOADS]
+
+        def load_g(part):
+            r0, r1, j0, j1 = G_LOADS[part]
+            nc.sync.dma_start(out=g_tiles[part][:], in_=g_rows[:, r0:r1, j0:j1])
+
+        load_g(0)
         nc.sync.dma_start(offsets[:], offs)
-        nc.gpsimd.dma_start(out=wb_raw[:].bitcast(I32), in_=wb_words[0].bitcast(I32))
+        load_g(1)
         for quad in range(QUADS):
             load_scales(nc.sync, wb_sc_raw, wb_scales, quad)
+        load_g(2)
+
+        def g_slice(r, a, b):
+            for (r0, r1, j0, j1), g_part in zip(G_LOADS, g_tiles):
+                if r0 <= r < r1 and j0 <= a and b <= j1:
+                    return g_part[:, r - r0, a - j0 : b - j0]
+            raise ValueError("no load holds this part of g")
 
         w_codes = sb("w_codes", [P, PACK, P], I32)
         w_sc = sb("w_sc", [P, PACK, P], U8)
@@ -80,24 +96,6 @@ def tile_list_pair_product_back_pl_kernel(
         nc.vector.tensor_copy(
             out=w_codes[:].rearrange("p r q -> p q r"), in_=w_raw[:].rearrange("p (q r) -> p q r", r=PACK)
         )
-
-        g_rows = g.rearrange("(p r) j -> p r j", r=PACK)
-        g_all = sb("g_all", [P, PACK * J], F32, tag="w_raw")
-        g_parts = []
-        start = 0
-        for r0, r1, j0, j1 in G_LOADS:
-            size = (r1 - r0) * (j1 - j0)
-            g_part = g_all[:, start : start + size].rearrange("p (r j) -> p r j", r=r1 - r0)
-            nc.sync.dma_start(out=g_part, in_=g_rows[:, r0:r1, j0:j1])
-            g_parts.append(start)
-            start = start + size
-
-        def g_slice(r, a, b):
-            for (r0, r1, j0, j1), first in zip(G_LOADS, g_parts):
-                if r0 <= r < r1 and j0 <= a and b <= j1:
-                    col = first + (r - r0) * (j1 - j0) + a - j0
-                    return g_all[:, col : col + b - a]
-            raise ValueError("no load holds this part of g")
 
         z_tiles = []
         for r in range(PACK):
@@ -117,15 +115,12 @@ def tile_list_pair_product_back_pl_kernel(
                 nc.scalar.copy(out=z[:, t0 : t0 + width], in_=z_bank[:])
             z_tiles.append(z)
 
-        wb_codes = sb("wb_codes", [P, PACK, 2 * P], U8, tag="w_sc_raw")
-        wb_sc = sb("wb_sc", [P, PACK, P], U8)
+        wb_codes = sb("wb_codes", [P, PACK, 2 * P], U8)
         nc.vector.tensor_copy(
             out=wb_codes[:].rearrange("p r (q b) -> p q r b", b=2),
             in_=wb_raw[:].rearrange("p (q r b) -> p q r b", r=PACK, b=2),
         )
 
-        d_codes = sb("d_codes", [P, J], U32)
-        d_sc = sb("d_sc", [P, J], U8)
         rounded = []
         for a, b in PIECES:
             d = sb("d%d" % a, [P, PACK, b - a], F32)
@@ -139,9 +134,12 @@ def tile_list_pair_product_back_pl_kernel(
             d_bf = sb("d_bf%d" % a, [P, b - a, PACK], BF16)
             interleave(nc.scalar.copy, d_bf[:], d[:])
             rounded.append(d_bf)
+        wb_sc = sb("wb_sc", [P, PACK, P], U8, tag="z%d" % (PACK - 1))
         nc.vector.tensor_copy(
             out=wb_sc[:].rearrange("p r q -> p q r"), in_=wb_sc_raw[:].rearrange("p (q r) -> p q r", r=PACK)
         )
+        d_codes = sb("d_codes", [P, J], U32, tag="g_0_256")
+        d_sc = sb("d_sc", [P, J], U8)
         for (a, b), d_bf in zip(PIECES, rounded):
             nc.vector.quantize_mx(
                 out=d_codes[:, a:b].bitcast(E5M2X4),

@@ -62,12 +62,12 @@ def tile_list_pair_product_back_pl_kernel(
             queue.dma_start(out=scale_rows(plane, quad), in_=src[0].bitcast(I32)[4 * quad : 4 * quad + 4, :])
 
         nc.sync.dma_start(out=xt_codes[:].bitcast(I32), in_=xt_words[0].bitcast(I32))
-        nc.sync.dma_start(out=w_raw[:], in_=w_words[0].rearrange("p n t -> p (n t)").bitcast(I32))
         for quad in range(QUADS):
             load_scales(nc.scalar if quad < 3 else nc.sync, w_sc_raw, w_scales, quad)
+        nc.sync.dma_start(out=w_raw[:], in_=w_words[0].rearrange("p n t -> p (n t)").bitcast(I32))
+        nc.sync.dma_start(out=wb_raw[:].bitcast(I32), in_=wb_words[0].bitcast(I32))
         for quad in range(QUADS):
             load_scales(nc.scalar if quad == 0 else nc.sync, xt_sc, xt_scales, quad)
-        nc.sync.dma_start(out=wb_raw[:].bitcast(I32), in_=wb_words[0].bitcast(I32))
         g_rows = g.rearrange("(p r) j -> p r j", r=PACK)
         g_tiles = [sb("g_%d_%d" % (r0, j0), [P, r1 - r0, j1 - j0], F32) for r0, r1, j0, j1 in G_LOADS]
 

@@ -18,23 +18,33 @@ MULT = mybir.AluOpType.mult
 
 P = 128
 PACK = 4
+PAIR = 2
 QUADS = 4
+QUAD_PARTITIONS = 32
+QUAD_SCALE_ROWS = 4
 LIST_ROWS = 16
-PIECES = ((0, 256), (256, 384), (384, 512))
-G_LOADS = ((0, 2, 0, 256), (2, 4, 0, 256), (0, 4, 256, 512))
-Y_HALF = 256
-Y_SPLIT = 96
+HALF = J // 2
+SPARE = 16
+VECTOR_SHARE = 128
+G_PARTS = ((0, 1, 0, J), (1, 2, 0, J), (2, PACK, 0, HALF), (2, PACK, HALF, J))
 
 
-def scale_rows(tile, quad):
-    return tile[32 * quad : 32 * quad + 4, :].bitcast(I32)
+def scale_rows(plane, quad):
+    first = QUAD_PARTITIONS * quad
+    return plane[first : first + QUAD_SCALE_ROWS, :].bitcast(I32)
 
 
-def interleave(copy, dst, src):
-    copy(
-        out=dst.rearrange("p (c i) t -> p c t i", i=4),
-        in_=src.rearrange("p t (c i) -> p c t i", i=4),
-    )
+def dram_scale_rows(scales, quad):
+    first = QUAD_SCALE_ROWS * quad
+    return scales[0].bitcast(I32)[first : first + QUAD_SCALE_ROWS, :]
+
+
+def deal(nc, dealt, raw):
+    nc.vector.tensor_copy(out=dealt.rearrange("p r q -> p q r"), in_=raw.rearrange("p (q r) -> p q r", r=PACK))
+
+
+def round_pair(copy, rounded, planes):
+    copy(out=rounded, in_=planes.rearrange("p r j -> p j r"))
 
 
 def tile_list_pair_product_back_pl_kernel(
@@ -55,51 +65,44 @@ def tile_list_pair_product_back_pl_kernel(
         w_sc_raw = sb("w_sc_raw", [P, N], U8)
         xt_sc = sb("xt_sc", [P, T], U8)
         wb_sc_raw = sb("wb_sc_raw", [P, M], U8)
-        for plane in (w_sc_raw, xt_sc, wb_sc_raw):
-            nc.vector.memset(plane[:].bitcast(I32), 0)
+        for scale_tile in (w_sc_raw, xt_sc, wb_sc_raw):
+            nc.vector.memset(scale_tile[:].bitcast(I32), 0)
 
-        def load_scales(queue, plane, src, quad):
-            queue.dma_start(out=scale_rows(plane, quad), in_=src[0].bitcast(I32)[4 * quad : 4 * quad + 4, :])
+        def load_scales(queue, scale_tile, scales, quad):
+            queue.dma_start(out=scale_rows(scale_tile, quad), in_=dram_scale_rows(scales, quad))
 
         nc.sync.dma_start(out=xt_codes[:].bitcast(I32), in_=xt_words[0].bitcast(I32))
         for quad in range(QUADS):
-            load_scales(nc.scalar if quad < 3 else nc.sync, w_sc_raw, w_scales, quad)
-        nc.sync.dma_start(out=w_raw[:], in_=w_words[0].rearrange("p n t -> p (n t)").bitcast(I32))
+            load_scales(nc.scalar if quad < QUADS - 1 else nc.sync, w_sc_raw, w_scales, quad)
+        nc.sync.dma_start(out=w_raw[:], in_=w_words[0].rearrange("p n r -> p (n r)").bitcast(I32))
         nc.sync.dma_start(out=wb_raw[:].bitcast(I32), in_=wb_words[0].bitcast(I32))
         for quad in range(QUADS):
             load_scales(nc.scalar if quad == 0 else nc.sync, xt_sc, xt_scales, quad)
-        g_rows = g.rearrange("(p r) j -> p r j", r=PACK)
-        g_tiles = [sb("g_%d_%d" % (r0, j0), [P, r1 - r0, j1 - j0], F32) for r0, r1, j0, j1 in G_LOADS]
+        g_planes = g.rearrange("(p r) j -> p r j", r=PACK)
+        g_tiles = [sb("g_%d_%d" % (r0, j0), [P, r1 - r0, j1 - j0], F32) for r0, r1, j0, j1 in G_PARTS]
 
         def load_g(part):
-            r0, r1, j0, j1 = G_LOADS[part]
-            nc.sync.dma_start(out=g_tiles[part][:], in_=g_rows[:, r0:r1, j0:j1])
+            r0, r1, j0, j1 = G_PARTS[part]
+            nc.sync.dma_start(out=g_tiles[part][:], in_=g_planes[:, r0:r1, j0:j1])
 
         load_g(0)
         nc.sync.dma_start(offsets[:], offs)
         load_g(1)
+        load_g(2)
         for quad in range(QUADS):
             load_scales(nc.sync, wb_sc_raw, wb_scales, quad)
-        load_g(2)
-
-        def g_slice(r, a, b):
-            for (r0, r1, j0, j1), g_part in zip(G_LOADS, g_tiles):
-                if r0 <= r < r1 and j0 <= a and b <= j1:
-                    return g_part[:, r - r0, a - j0 : b - j0]
-            raise ValueError("no load holds this part of g")
+        load_g(3)
 
         w_codes = sb("w_codes", [P, PACK, P], I32)
         w_sc = sb("w_sc", [P, PACK, P], U8)
-        nc.vector.tensor_copy(
-            out=w_sc[:].rearrange("p r q -> p q r"), in_=w_sc_raw[:].rearrange("p (q r) -> p q r", r=PACK)
-        )
-        nc.vector.tensor_copy(
-            out=w_codes[:].rearrange("p r q -> p q r"), in_=w_raw[:].rearrange("p (q r) -> p q r", r=PACK)
-        )
+        deal(nc, w_sc[:], w_sc_raw[:])
+        deal(nc, w_codes[:], w_raw[:])
 
-        z_tiles = []
+        z_planes = []
         for r in range(PACK):
-            z = sb("z%d" % r, [P, T], F32)
+            z = sb("z%d" % r, [P, T + SPARE if r < PAIR else T], F32)
+            if r < PAIR:
+                nc.vector.memset(z[:, T:], 0.0)
             width = T // 2 if r == 0 else T
             for t0 in range(0, T, width):
                 z_bank = psum.tile([P, width], F32, name="z_bank%d_%d" % (r, t0))
@@ -113,7 +116,7 @@ def tile_list_pair_product_back_pl_kernel(
                     stop=True,
                 )
                 nc.scalar.copy(out=z[:, t0 : t0 + width], in_=z_bank[:])
-            z_tiles.append(z)
+            z_planes.append(z)
 
         wb_codes = sb("wb_codes", [P, PACK, 2 * P], U8)
         nc.vector.tensor_copy(
@@ -121,37 +124,41 @@ def tile_list_pair_product_back_pl_kernel(
             in_=wb_raw[:].rearrange("p (q r b) -> p q r b", r=PACK, b=2),
         )
 
-        rounded = []
-        for a, b in PIECES:
-            d = sb("d%d" % a, [P, PACK, b - a], F32)
-            for r in range(PACK):
+        halves = [slice(h * HALF, (h + 1) * HALF) for h in range(2)]
+        d_low = sb("d_low", [P, PAIR, J], F32)
+        d_high = [sb("d_high%d" % h, [P, PAIR, HALF], F32) for h in range(2)]
+        d_bf = [sb("d_bf%d" % h, [P, HALF, PACK], BF16) for h in range(2)]
+        for r in range(PAIR):
+            nc.vector.tensor_tensor(d_low[:, r, :], z_planes[r][:].indirect(offsets[:]), g_tiles[r][:, 0, :], MULT)
+        for h in range(2):
+            round_pair(nc.scalar.copy, d_bf[h][:, :, :PAIR], d_low[:, :, halves[h]])
+        for h in range(2):
+            list_half = offsets[:, halves[h].start // LIST_ROWS : halves[h].stop // LIST_ROWS]
+            for r in range(PAIR, PACK):
                 nc.vector.tensor_tensor(
-                    d[:, r, :],
-                    z_tiles[r][:].indirect(offsets[:, a // LIST_ROWS : b // LIST_ROWS]),
-                    g_slice(r, a, b),
+                    d_high[h][:, r - PAIR, :],
+                    z_planes[r][:].indirect(list_half),
+                    g_tiles[PAIR + h][:, r - PAIR, :],
                     MULT,
                 )
-            d_bf = sb("d_bf%d" % a, [P, b - a, PACK], BF16)
-            interleave(nc.scalar.copy, d_bf[:], d[:])
-            rounded.append(d_bf)
+        round_pair(nc.scalar.copy, d_bf[0][:, :, PAIR:], d_high[0][:])
+        round_pair(nc.scalar.copy, d_bf[1][:, VECTOR_SHARE:, PAIR:], d_high[1][:, :, VECTOR_SHARE:])
         wb_sc = sb("wb_sc", [P, PACK, P], U8, tag="z%d" % (PACK - 1))
-        nc.vector.tensor_copy(
-            out=wb_sc[:].rearrange("p r q -> p q r"), in_=wb_sc_raw[:].rearrange("p (q r) -> p q r", r=PACK)
-        )
-        d_codes = sb("d_codes", [P, J], U32, tag="g_0_256")
+        deal(nc, wb_sc[:], wb_sc_raw[:])
+        round_pair(nc.vector.tensor_copy, d_bf[1][:, :VECTOR_SHARE, PAIR:], d_high[1][:, :, :VECTOR_SHARE])
+        d_codes = sb("d_codes", [P, J], U32, tag="g_%d_%d" % (PAIR, HALF))
         d_sc = sb("d_sc", [P, J], U8)
-        for (a, b), d_bf in zip(PIECES, rounded):
+        for h in range(2):
             nc.vector.quantize_mx(
-                out=d_codes[:, a:b].bitcast(E5M2X4),
-                scales=d_sc[:, a:b],
-                in_=d_bf[:].rearrange("p j t -> p (j t)"),
+                out=d_codes[:, halves[h]].bitcast(E5M2X4),
+                scales=d_sc[:, halves[h]],
+                in_=d_bf[h][:].rearrange("p j r -> p (j r)"),
             )
 
-        out_rows = out_0.rearrange("(p r) j -> p r j", r=PACK)
-        halves = [slice(h * Y_HALF, (h + 1) * Y_HALF) for h in range(2)]
-        y_low = sb("y_low", [P, 2, J], F32)
-        y_high = [sb("y_high%d" % h, [P, 2, Y_HALF], F32) for h in range(2)]
-        y_bf = [sb("y_bf%d" % h, [P, Y_HALF, PACK], BF16) for h in range(2)]
+        out_planes = out_0.rearrange("(p r) j -> p r j", r=PACK)
+        y_low = sb("y_low", [P, PAIR, J], F32)
+        y_high = [sb("y_high%d" % h, [P, PAIR, HALF], F32) for h in range(2)]
+        y_bf = [sb("y_bf%d" % h, [P, HALF, PACK], BF16) for h in range(2)]
         for r in range(PACK):
             y_bank = psum.tile([P, J], F32, name="y_bank%d" % r, tag="z_bank0_0" if r == PACK - 1 else "y_bank%d" % r)
             nc.tensor.matmul_mx(
@@ -163,33 +170,32 @@ def tile_list_pair_product_back_pl_kernel(
                 start=True,
                 stop=True,
             )
-            if r < 2:
+            if r < PAIR:
                 copy = nc.vector.tensor_copy if r == 0 else nc.scalar.copy
                 copy(out=y_low[:, r, :], in_=y_bank[:])
-                nc.sync.dma_start(out=out_rows[:, r, :], in_=y_low[:, r, :])
+                nc.sync.dma_start(out=out_planes[:, r, :], in_=y_low[:, r, :])
             else:
                 for h in range(2):
-                    nc.scalar.copy(out=y_high[h][:, r - 2, :], in_=y_bank[:, halves[h]])
-            if r == 1:
+                    nc.scalar.copy(out=y_high[h][:, r - PAIR, :], in_=y_bank[:, halves[h]])
+            if r == PAIR - 1:
                 for h in range(2):
-                    nc.vector.tensor_copy(out=y_bf[h][:, :, 0:2], in_=y_low[:, :, halves[h]].rearrange("p t j -> p j t"))
+                    round_pair(nc.vector.tensor_copy, y_bf[h][:, :, :PAIR], y_low[:, :, halves[h]])
         for h in range(2):
-            nc.sync.dma_start(out=out_rows[:, 2:PACK, halves[h]], in_=y_high[h][:])
-        nc.vector.tensor_copy(out=y_bf[0][:, :, 2:PACK], in_=y_high[0][:].rearrange("p t j -> p j t"))
-        nc.scalar.copy(out=y_bf[1][:, Y_SPLIT:, 2:PACK], in_=y_high[1][:, :, Y_SPLIT:].rearrange("p t j -> p j t"))
-        nc.vector.tensor_copy(out=y_bf[1][:, :Y_SPLIT, 2:PACK], in_=y_high[1][:, :, :Y_SPLIT].rearrange("p t j -> p j t"))
+            nc.sync.dma_start(out=out_planes[:, PAIR:, halves[h]], in_=y_high[h][:])
+        round_pair(nc.vector.tensor_copy, y_bf[0][:, :, PAIR:], y_high[0][:])
+        round_pair(nc.scalar.copy, y_bf[1][:, VECTOR_SHARE:, PAIR:], y_high[1][:, :, VECTOR_SHARE:])
+        round_pair(nc.vector.tensor_copy, y_bf[1][:, :VECTOR_SHARE, PAIR:], y_high[1][:, :, :VECTOR_SHARE])
 
         y_codes = sb("y_codes", [P, J], U32)
         y_sc = sb("y_sc", [P, J], U8)
-        words_out = out_1[0].rearrange("p c t -> p (c t)").bitcast(I32)
+        words_out = out_1[0].rearrange("p j r -> p (j r)").bitcast(I32)
         for h in range(2):
-            cols = slice(h * Y_HALF, (h + 1) * Y_HALF)
             nc.vector.quantize_mx(
-                out=y_codes[:, cols].bitcast(E4M3X4),
-                scales=y_sc[:, cols],
-                in_=y_bf[h][:].rearrange("p j t -> p (j t)"),
+                out=y_codes[:, halves[h]].bitcast(E4M3X4),
+                scales=y_sc[:, halves[h]],
+                in_=y_bf[h][:].rearrange("p j r -> p (j r)"),
             )
-            nc.sync.dma_start(out=words_out[:, cols], in_=y_codes[:, cols].bitcast(I32))
+            nc.sync.dma_start(out=words_out[:, halves[h]], in_=y_codes[:, halves[h]].bitcast(I32))
         for quad in range(QUADS):
-            queue = nc.scalar if quad < 3 else nc.sync
-            queue.dma_start(out=out_2[0].bitcast(I32)[4 * quad : 4 * quad + 4, :], in_=scale_rows(y_sc, quad))
+            queue = nc.scalar if quad < QUADS - 1 else nc.sync
+            queue.dma_start(out=dram_scale_rows(out_2, quad), in_=scale_rows(y_sc, quad))

from contextlib import ExitStack

import concourse.mybir as mybir

K, N, M, T, J = 512, 512, 512, 512, 512
FLOPS = 2 * K * N * T + 2 * N * M * J

F32 = mybir.dt.float32
BF16 = mybir.dt.bfloat16
I32 = mybir.dt.int32
U32 = mybir.dt.uint32
U16 = mybir.dt.uint16
U8 = mybir.dt.uint8
E4M3X4 = mybir.dt.float8_e4m3fn_x4
E5M2X4 = mybir.dt.float8_e5m2_x4
E2M1X4 = mybir.dt.float4_e2m1fn_x4
MULT = mybir.AluOpType.mult

P = 128
PACK = 4
PAIR = 2
QUADS = 4
QUAD_PARTITIONS = 32
QUAD_SCALE_ROWS = 4
LIST_ROWS = 16
HALF = J // 2
SPARE = 16
VECTOR_SHARE = 128
G_PARTS = ((0, 1, 0, J), (1, 2, 0, J), (2, PACK, 0, HALF), (2, PACK, HALF, J))


def scale_rows(plane, quad):
    first = QUAD_PARTITIONS * quad
    return plane[first : first + QUAD_SCALE_ROWS, :].bitcast(I32)


def dram_scale_rows(scales, quad):
    first = QUAD_SCALE_ROWS * quad
    return scales[0].bitcast(I32)[first : first + QUAD_SCALE_ROWS, :]


def deal(nc, dealt, raw):
    nc.vector.tensor_copy(out=dealt.rearrange("p r q -> p q r"), in_=raw.rearrange("p (q r) -> p q r", r=PACK))


def round_pair(copy, rounded, planes):
    copy(out=rounded, in_=planes.rearrange("p r j -> p j r"))


def tile_list_pair_product_back_pl_kernel(
    tc, xt_words, xt_scales, w_words, w_scales, g, wb_words, wb_scales, offs, out_0, out_1, out_2
):
    nc = tc.nc
    with ExitStack() as ctx:
        keep = ctx.enter_context(tc.tile_pool(name="keep", bufs=1))
        psum = ctx.enter_context(tc.psum_pool(name="psum", bufs=1))

        def sb(name, shape, dtype, tag=None):
            return keep.tile(shape, dtype, name=name, tag=tag or name, align_bytes=64)

        offsets = keep.tile([P, J // LIST_ROWS], U16, name="offsets")
        w_raw = sb("w_raw", [P, N], I32)
        xt_codes = sb("xt_codes", [P, 2 * T], U8)
        wb_raw = sb("wb_raw", [P, 2 * M], U8)
        w_sc_raw = sb("w_sc_raw", [P, N], U8)
        xt_sc = sb("xt_sc", [P, T], U8)
        wb_sc_raw = sb("wb_sc_raw", [P, M], U8)
        for scale_tile in (w_sc_raw, xt_sc, wb_sc_raw):
            nc.vector.memset(scale_tile[:].bitcast(I32), 0)

        def load_scales(queue, scale_tile, scales, quad):
            queue.dma_start(out=scale_rows(scale_tile, quad), in_=dram_scale_rows(scales, quad))

        nc.sync.dma_start(out=xt_codes[:].bitcast(I32), in_=xt_words[0].bitcast(I32))
        for quad in range(QUADS):
            load_scales(nc.scalar if quad < QUADS - 1 else nc.sync, w_sc_raw, w_scales, quad)
        nc.sync.dma_start(out=w_raw[:], in_=w_words[0].rearrange("p n r -> p (n r)").bitcast(I32))
        nc.sync.dma_start(out=wb_raw[:].bitcast(I32), in_=wb_words[0].bitcast(I32))
        for quad in range(QUADS):
            load_scales(nc.scalar if quad == 0 else nc.sync, xt_sc, xt_scales, quad)
        g_planes = g.rearrange("(p r) j -> p r j", r=PACK)
        g_tiles = [sb("g_%d_%d" % (r0, j0), [P, r1 - r0, j1 - j0], F32) for r0, r1, j0, j1 in G_PARTS]

        def load_g(part):
            r0, r1, j0, j1 = G_PARTS[part]
            nc.sync.dma_start(out=g_tiles[part][:], in_=g_planes[:, r0:r1, j0:j1])

        load_g(0)
        nc.sync.dma_start(offsets[:], offs)
        load_g(1)
        load_g(2)
        for quad in range(QUADS):
            load_scales(nc.sync, wb_sc_raw, wb_scales, quad)
        load_g(3)

        w_codes = sb("w_codes", [P, PACK, P], I32)
        w_sc = sb("w_sc", [P, PACK, P], U8)
        deal(nc, w_sc[:], w_sc_raw[:])
        deal(nc, w_codes[:], w_raw[:])

        z_planes = []
        for r in range(PACK):
            z = sb("z%d" % r, [P, T + SPARE if r < PAIR else T], F32)
            if r < PAIR:
                nc.vector.memset(z[:, T:], 0.0)
            width = T // 2 if r == 0 else T
            for t0 in range(0, T, width):
                z_bank = psum.tile([P, width], F32, name="z_bank%d_%d" % (r, t0))
                nc.tensor.matmul_mx(
                    out=z_bank[:],
                    lhsT=w_codes[:, r, :].bitcast(E4M3X4),
                    lhsT_scale=w_sc[:, r, :],
                    rhs=xt_codes[:, 2 * t0 : 2 * (t0 + width)].bitcast(E2M1X4),
                    rhs_scale=xt_sc[:, t0 : t0 + width],
                    start=True,
                    stop=True,
                )
                nc.scalar.copy(out=z[:, t0 : t0 + width], in_=z_bank[:])
            z_planes.append(z)

        wb_codes = sb("wb_codes", [P, PACK, 2 * P], U8)
        nc.vector.tensor_copy(
            out=wb_codes[:].rearrange("p r (q b) -> p q r b", b=2),
            in_=wb_raw[:].rearrange("p (q r b) -> p q r b", r=PACK, b=2),
        )

        halves = [slice(h * HALF, (h + 1) * HALF) for h in range(2)]
        d_low = sb("d_low", [P, PAIR, J], F32)
        d_high = [sb("d_high%d" % h, [P, PAIR, HALF], F32) for h in range(2)]
        d_bf = [sb("d_bf%d" % h, [P, HALF, PACK], BF16) for h in range(2)]
        for r in range(PAIR):
            nc.vector.tensor_tensor(d_low[:, r, :], z_planes[r][:].indirect(offsets[:]), g_tiles[r][:, 0, :], MULT)
        for h in range(2):
            round_pair(nc.scalar.copy, d_bf[h][:, :, :PAIR], d_low[:, :, halves[h]])
        for h in range(2):
            list_half = offsets[:, halves[h].start // LIST_ROWS : halves[h].stop // LIST_ROWS]
            for r in range(PAIR, PACK):
                nc.vector.tensor_tensor(
                    d_high[h][:, r - PAIR, :],
                    z_planes[r][:].indirect(list_half),
                    g_tiles[PAIR + h][:, r - PAIR, :],
                    MULT,
                )
        round_pair(nc.scalar.copy, d_bf[0][:, :, PAIR:], d_high[0][:])
        round_pair(nc.scalar.copy, d_bf[1][:, VECTOR_SHARE:, PAIR:], d_high[1][:, :, VECTOR_SHARE:])
        wb_sc = sb("wb_sc", [P, PACK, P], U8, tag="z%d" % (PACK - 1))
        deal(nc, wb_sc[:], wb_sc_raw[:])
        round_pair(nc.vector.tensor_copy, d_bf[1][:, :VECTOR_SHARE, PAIR:], d_high[1][:, :, :VECTOR_SHARE])
        d_codes = sb("d_codes", [P, J], U32, tag="g_%d_%d" % (PAIR, HALF))
        d_sc = sb("d_sc", [P, J], U8)
        for h in range(2):
            nc.vector.quantize_mx(
                out=d_codes[:, halves[h]].bitcast(E5M2X4),
                scales=d_sc[:, halves[h]],
                in_=d_bf[h][:].rearrange("p j r -> p (j r)"),
            )

        out_planes = out_0.rearrange("(p r) j -> p r j", r=PACK)
        y_low = sb("y_low", [P, PAIR, J], F32)
        y_high = [sb("y_high%d" % h, [P, PAIR, HALF], F32) for h in range(2)]
        y_bf = [sb("y_bf%d" % h, [P, HALF, PACK], BF16) for h in range(2)]
        for r in range(PACK):
            y_bank = psum.tile([P, J], F32, name="y_bank%d" % r, tag="z_bank0_0" if r == PACK - 1 else "y_bank%d" % r)
            nc.tensor.matmul_mx(
                out=y_bank[:],
                lhsT=wb_codes[:, r, :].bitcast(E2M1X4),
                lhsT_scale=wb_sc[:, r, :],
                rhs=d_codes[:].bitcast(E5M2X4),
                rhs_scale=d_sc[:],
                start=True,
                stop=True,
            )
            if r < PAIR:
                copy = nc.vector.tensor_copy if r == 0 else nc.scalar.copy
                copy(out=y_low[:, r, :], in_=y_bank[:])
                nc.sync.dma_start(out=out_planes[:, r, :], in_=y_low[:, r, :])
            else:
                for h in range(2):
                    nc.scalar.copy(out=y_high[h][:, r - PAIR, :], in_=y_bank[:, halves[h]])
            if r == PAIR - 1:
                for h in range(2):
                    round_pair(nc.vector.tensor_copy, y_bf[h][:, :, :PAIR], y_low[:, :, halves[h]])
        for h in range(2):
            nc.sync.dma_start(out=out_planes[:, PAIR:, halves[h]], in_=y_high[h][:])
        round_pair(nc.vector.tensor_copy, y_bf[0][:, :, PAIR:], y_high[0][:])
        round_pair(nc.scalar.copy, y_bf[1][:, VECTOR_SHARE:, PAIR:], y_high[1][:, :, VECTOR_SHARE:])
        round_pair(nc.vector.tensor_copy, y_bf[1][:, :VECTOR_SHARE, PAIR:], y_high[1][:, :, :VECTOR_SHARE])

        y_codes = sb("y_codes", [P, J], U32)
        y_sc = sb("y_sc", [P, J], U8)
        words_out = out_1[0].rearrange("p j r -> p (j r)").bitcast(I32)
        for h in range(2):
            nc.vector.quantize_mx(
                out=y_codes[:, halves[h]].bitcast(E4M3X4),
                scales=y_sc[:, halves[h]],
                in_=y_bf[h][:].rearrange("p j r -> p (j r)"),
            )
            nc.sync.dma_start(out=words_out[:, halves[h]], in_=y_codes[:, halves[h]].bitcast(I32))
        for quad in range(QUADS):
            queue = nc.scalar if quad < QUADS - 1 else nc.sync
            queue.dma_start(out=dram_scale_rows(out_2, quad), in_=scale_rows(y_sc, quad))
